import numpy as np, ml_dtypes
CORES = [3,11,19,27,35,43]
N = 6
BF = ml_dtypes.bfloat16
W, I, B, S, RO, H = 8192, 64, 128, 8, 4, 10
def some(rng, k):
    o = np.argsort(rng.random(k.shape[:-1] + (16,) + k.shape[-1:]), axis=-2)
    return np.where(o < k[..., None, :], 0, 255)
def parts(rng):
    x = rng.integers(0, 256, (N, 8, 16, W)); w = rng.integers(0, 16, (N, 8, 16, 1)); c = rng.integers(0, 128, (N, 8, 16, I))
    l = rng.integers(1, 5, (N, 8, 16, I)); s = rng.integers(0, W, (N, 8, 16, I))
    v = rng.choice(np.array([96, 176, 208, 224, 236, 244, 252]), (N, 8, 1, I))
    return x, w, c, l, s, np.clip(v + rng.integers(-12, 13, (N, 8, 16, I)), 0, 255)
def small(a):
    return np.ascontiguousarray(a.reshape(N, 128, -1)).astype(np.float32).astype(BF)
def pack(x, w, c, l, s, fl):
    return {"x": small(x), "wt": small(w), "ch": small(c), "sp": small(l), "st": np.ascontiguousarray(s.reshape(N, 128, I)).astype(np.int32), "fl": small(fl)}
def setup_inputs(rng):
    return pack(*parts(rng))
def setup_inputs_spread(rng):
    x, w, c, l, s, fl = parts(rng)
    x = (np.exp2(8 * rng.random((N, 8, 1, W))) * rng.random(x.shape)).astype(np.int64)
    w = np.where(rng.random(w.shape) < 0.4, 0, w)
    c = np.where(rng.random((N, 8, 1, I)) < 0.5, c, np.exp2(7 * rng.random(c.shape)).astype(np.int64) - 1)
    l = rng.choice(np.array([1, 1, 1, 2, 3, 4]), l.shape)
    fl = (np.exp2(8 * rng.random((N, 8, 1, I))) * (0.5 + 0.5 * rng.random(fl.shape))).astype(np.int64)
    return pack(x, w, c, l, s, fl)
def setup_inputs_ends(rng):
    x, w, c, l, s, fl = parts(rng)
    d = rng.choice(np.array([0.04, 0.1, 0.3, 0.5]), (N, 8, 1, 1)); d[:, 7] = 0.5
    e = 255 * (rng.random(x.shape) < d); k = rng.random((N, 8, 1, W)); full = np.where(np.arange(8) == 7, 0.3, 0.03).reshape(1, 8, 1, 1)
    e = np.where(k < full, 255, np.where(k > 0.85, 0, e)); x = np.where((k > 0.5) & (k < 0.6), x, e)
    w = 15 * rng.integers(0, 2, w.shape); w[:, 7] = 15; w[:, 1] = 0; w[:, 0, 0] = 0; w[:, 0, 15] = 15
    b = rng.random((N, 8, 1, I)); c = np.where(b < 0.15, 127, np.where(b > 0.85, 0, 127 * rng.integers(0, 2, c.shape)))
    l = 1 + 3 * rng.integers(0, 2, l.shape); s = np.where(rng.random(s.shape) < 0.25, s, (W - 1) * rng.integers(0, 2, s.shape))
    fl = some(rng, rng.integers(0, 17, (N, 8, I))); fl[N - 2:] = some(rng, rng.integers(H, 17, (2, 8, I)))
    x[N - 2, 6, H - 1:] = 0; fl[N - 2, 6, :, I - 1] = np.where(np.arange(16) < H - 1, 0, 255)
    l[N - 1, 7, :, :2] = 4; s[N - 1, 7, :, :2] = W - 1
    l[N - 1, 7, 13:, I - 1] = np.array([1, 4, 4]); s[N - 1, 7, 13:, I - 1] = np.array([(0 - 613) & (W - 1), (W - 1 - 2452) & (W - 1), W - 1])
    c[N - 1, 7, 0, :2] = 127; c[N - 1, 7, 0, I - 1] = 127
    x[:, 7, :, (W - 1 + 2452) & (W - 1)] = 255; x[:, 7, :, W - 1] = 255; x[:, 7, 15] = 255
    return pack(x, w, c, l, s, fl)
def setup_inputs_corners(rng):
    x, w, c, l, s, fl = parts(rng); q = rng.permutation(N); ar = np.arange(16)[:, None]
    w[:, 0] = 0; b = rng.integers(0, 4, (N, 1, I)); c[:, 0] = np.where(b == 0, 3, np.where(b == 1, 0, np.where(b == 2, 127, c[:, 0])))
    x[:, 1] = np.minimum(x[:, 1], 254); fl[:, 1] = some(rng, rng.choice(np.array([0, H - 1, H, 16]), (N, I)))
    v = rng.integers(1, 255, (N, 16, 1)); x[:, 2] = v; fl[:, 2] = v + np.minimum(some(rng, rng.choice(np.array([H - 1, H, 16]), (N, I))), 1)
    w[:, 3] = 0; w[:, 3, 0] = 1; x[:, 3, 0, ::2] = 255; fl[:, 3] = fl[:, 3] // 2
    b = rng.integers(0, 4, (N, 1, I)); l[:, 4] = np.where(b == 0, 4, np.where(b == 1, 1, np.where(b == 2, 1 + 3 * (ar == 15), 1 + 3 * (ar & 1)))); fl[:, 4] = fl[:, 4] // 2
    e = (W - 1) * rng.integers(0, 2, (N, 16, I)); s[:, 5] = np.where(rng.random((N, 16, I)) < 0.5, e, (e - 613 * l[:, 5]) & (W - 1))
    w[:, 6] = 15; x[:, 6] = rng.integers(224, 256, (N, 16, W)); c[:, 6] = rng.choice(np.array([0, 126, 127]), (N, 16, I))
    x[q[0]] = np.minimum(x[q[0]], 254); fl[q[0]] = some(rng, np.full((8, I), H - 1))
    fl[q[1]] = some(rng, rng.integers(H, 17, (8, I))); fl[q[2]] = some(rng, rng.integers(H, 17, (8, I)))
    x[q[2], 7] = np.minimum(x[q[2], 7], 254); fl[q[2], 7, :, I - 1] = some(rng, np.full(1, H - 1))[:, 0]
    return pack(x, w, c, l, s, fl)
def setup_inputs_crowd(rng):
    x, w, c, l, s, fl = parts(rng); q = rng.permutation(N)
    s[:, :7] = rng.integers(0, W, (N, 7, 1, 1)); l[:, :7] = rng.integers(1, 5, (N, 7, 1, 1)); c[:, :7] = rng.integers(0, 128, (N, 7, 16, 1))
    s[:, 4:7, 15, I - 1] = rng.integers(0, W, (N, 3)); c[:, 4:7, :, I - 1] = rng.integers(0, 128, (N, 3, 16))
    fl = some(rng, rng.integers(H, 17, (N, 8, I)))
    for a in q[:N // 2]:
        x[a, 7] = np.minimum(x[a, 7], 254); fl[a, 7, :, I - 1] = some(rng, np.full(1, H - 1))[:, 0]
    return pack(x, w, c, l, s, fl)
def setup_inputs_late(rng):
    x, w, c, l, s, fl = parts(rng); q = rng.permutation(N); a, b = int(q[0]), int(q[1])
    x[a] = np.minimum(x[a], 254); fl[a] = some(rng, np.full((8, I), H - 1)); fl[b] = some(rng, rng.integers(H, 17, (8, I)))
    for r, g, low in ((a, 7, 8), (b, 0, 0)):
        hot = B * int(rng.integers(8, I)); w[r, g] = 0
        x[r, g] = rng.integers(0, 101, (16, W)); x[r, g, :, hot] = rng.integers(200, 255, 16)
        fl[r, g, :, low:] = rng.integers(110, 151, (16, I - low))
        l[r, g] = 1; s[r, g] = (hot - 613) & (W - 1)
        if g == 7: l[(a - 2) % N, 7] = 1; s[(a - 2) % N, 7] = (hot - 613) & (W - 1)
    s[(a - 1) % N, 7] = (16 * rng.integers(0, W // 16, (16, I)) - (I - 8)) & (W - 1)
    l[(b - 1) % N, 0] = 1; s[(b - 1) % N, 0] = W - 613 - 8 * I
    c[(b - 1) % N, 0] = 16 * rng.integers(0, 8, (16, I)) + 4 * rng.integers(1, 4, (16, I))
    return pack(x, w, c, l, s, fl)
def check_inputs(d):
    bad = []
    for k, lo, hi in (("x", 0, 255), ("wt", 0, 15), ("ch", 0, 127), ("sp", 1, 4), ("st", 0, W - 1), ("fl", 0, 255)):
        v = np.asarray(d[k]).astype(np.float64)
        if not (np.all(v >= lo) and np.all(v <= hi)): bad.append("range of " + k)
        if np.any(v != np.floor(v)): bad.append("whole numbers of " + k)
    return bad
def reference(x, wt, ch, sp, st, fl):
    X, Q, C, L, Z, F = [v.astype(np.float32).astype(np.int32).reshape(N, 8, 16, -1) for v in (x, wt, ch, sp, st, fl)]
    A = [0] * N; row = np.arange(16)[:, None]
    for t in range(RO):
        if t > 0: C, L, Z = np.roll(C, 1, axis=0), np.roll(L, 1, axis=0), np.roll(Z, 1, axis=0)
        for a in range(N):
            l = L[a]
            at = np.arange(16)[None, :, None, None]; at = at + np.where(at >= row[None, None], l[:, None], 0)
            e = np.take_along_axis(np.concatenate([C[a], np.zeros((8, 4, I), np.int32)], axis=1)[:, :, None, :], at, 1)
            e = np.concatenate([e, np.zeros((8, 1, 16, I), np.int32)], axis=1)
            s = (Z[a] + 613 * l + A[a]) & (W - 1); p = np.zeros((8, 16, I), np.int64); V = np.zeros((8, 16, 16, I), np.int32); log = []
            for k in range(S):
                z = np.take_along_axis(X[a], s.reshape(8, 1, 16 * I), 2).reshape(8, 16, 16, I)
                V = np.maximum(V, z); c = np.take_along_axis(e, np.minimum(p, 16)[:, None], 1)[:, 0].astype(np.int64)
                u = np.add.reduce(Q[a][..., None] * z, axis=1).astype(np.int64)
                n = 1 + (((u >> 3) + c) & 3); log.append((p, n))
                s = (((u * (2 * c + 1)) >> 3) + 37 * u + c) & (W - 1); p = p + n
            fails = np.add.reduce((V >= F[a][:, :, None, :]).astype(np.int32), axis=1) >= H
            best = np.argmax(np.where(fails, 16 * l + 15 - row[None], 0 - 1), axis=1)[:, None, :]; ok = np.any(fails, axis=1)[:, None, :]
            nl = np.ones((8, 16, I), np.int64)
            for p, n in log: nl = np.where(row[None] == np.take_along_axis(p, best, 1), np.take_along_axis(n, best, 1), nl)
            v = np.take_along_axis(V, best[:, None], 2)[:, :, 0]
            C[a] = np.where(ok, np.take_along_axis(e[:, :16], best[:, None], 2)[:, :, 0], C[a]); L[a] = np.where(ok, nl, l)
            to = B * np.arange(I)[None, None, :] + (np.add.reduce(Q[a] * v, axis=1)[:, None, :] & (B - 1))
            to = np.broadcast_to(to, (8, 16, I)); np.put_along_axis(X[a], to, np.where(ok, v, np.take_along_axis(X[a], to, 2)), 2)
            F[a] = np.where(ok, (F[a] + v) >> 1, F[a]); A[a] = int(np.sum(ok))
    sums = np.add.reduce(X.reshape(N, 128, I, B), axis=3)
    return {"yc": C.reshape(N, 128, I).astype(np.float32).astype(BF), "yl": L.reshape(N, 128, I).astype(np.float32).astype(BF),
            "yf": F.reshape(N, 128, I).astype(np.float32).astype(BF), "ys": sums.astype(np.float32)}

from concourse.mybir import dt, AluOpType, AxisListType, ActivationFunctionType

ADD, SUB, MUL, MAX, MIN = AluOpType.add, AluOpType.subtract, AluOpType.mult, AluOpType.max, AluOpType.min
GE, EQ = AluOpType.is_ge, AluOpType.is_equal
SHR, AND = AluOpType.arith_shift_right, AluOpType.bitwise_and
IDT, SIGN = ActivationFunctionType.Identity, ActivationFunctionType.Sign
COPY = ActivationFunctionType.Copy
RO, S, W = 4, 8, 8192
DUMP = W + 64
RTW = 33 * 64

SCRATCH = {}
POOL = {}


def _d(names, cols, dtype, where="sbuf"):
    for n in names.split():
        SCRATCH[n] = (where, [128, cols], dtype)


def _pool(buf, names, cols, dtype):
    for k, n in enumerate(names.split()):
        POOL[n] = (buf, k * cols, cols)
    SCRATCH[buf] = ("sbuf", [128, len(names.split()) * cols], dtype)


_d("X", DUMP, "bfloat16")
_d("ZA OA ZB OB", 4096, "bfloat16")
_d("Z7 CB GEb", 1024, "bfloat16")
_d("VB", 1040, "bfloat16")
_d("RT", RTW, "bfloat16")
_d("Gm Dm Wm GT", 2048, "bfloat16")
_d("ID BO BO3 BO1 WB8 WB1 SH1 SH2 SH3 SH4 IN1 IN2 R0 NEG ON16 shx", 128, "bfloat16")
_d("ONE SC PX OK VV OLD DIF LM15", 64, "bfloat16")
_d("MASK4", 1024, "bfloat16")
_d("MASK16 SX", 128, "bfloat16")
_d("LOG OHL", 576, "bfloat16")
_d("KQ AT SG", 512, "bfloat16")
_d("MK CM", 256, "bfloat16")
_d("F0 F1 F2 F3 F4", 64, "bfloat16")
_d("LND0 LND1 LND2 LND3 SND0 SND1 SND2 SND3", 128, "bfloat16")
_d("WT", 1, "bfloat16")
_d("ST0 ST1 ST2 ST3", 64, "int32")
_pool("INTS", "SA I1 N64 DH YI SI T613 S0 BI LI MI HI HM FVI FH", 64, "int32")
_d("ROW CQI CGI", 128, "int32")
_d("KQI", 512, "int32")
_d("PI QI GI", 1, "int32")
_d("ROWF CQF CGF", 128, "float32")
_d("PC QC GC QC64 QN4 C16M ACOL", 1, "float32")
_d("PCL PCG", 4, "float32")
_d("EQ16", 16, "float32")
_d("MC", 8, "float32")
_pool("FLTS", "CA CBF PR M16F DIAG OFXC PRI FT GG LE DL MD SD X1 OKD X2 SD2 FD FE", 64, "float32")
_d("I4 BV4 BX4 O4 O4X", 4, "float32")
_d("L0 QS", 128, "float32")
_d("DP0 DP1 DP2 DP3 DP4 DP5 DP6 DP7", 128, "float32")
_d("YS", 64, "float32")
_d("OFFZ OFFC", 64, "uint16")
_d("OV OX", 4, "uint16")
_d("psF0 psF1 psW psC psA psB psY", 512, "float32", "psum")
_d("psT", 1024, "bfloat16", "psum")

SEMAPHORES = ["qv", "qs", "qt", "qg", "dX", "dW", "dC", "dL", "dS", "dF", "oC", "oL", "oF", "oS", "loc"]
SEMAPHORES += ["st%d" % t for t in range(1, RO)] + ["arr%d" % t for t in range(1, RO)]

C_SCALAR, Z_SCALAR, Z0_SCALAR = 38, 26, 38


class Ap(tuple):
    pass


def rank_program(g, core, T, topo):
    rank = T.rank_of(core)
    if rank is None:
        return
    n = len(T.cores)
    queue = {"v": g.vector, "s": g.scalar, "t": g.tensor, "g": g, "y": g.sync}
    count = {"v": 0, "s": 0, "t": 0, "g": 0}
    known = {q: {} for q in queue}
    snap = {}
    seen = {}

    def A(name, a=None, b=None, step=1, p=128):
        buf, off, cols = POOL[name] if name in POOL else (name, 0, SCRATCH[name][1][1])
        a = 0 if a is None else a
        b = cols if b is None else b
        ap = T[buf][0:p, off + a:off + b] if step == 1 else T[buf][0:p, off + a:off + b:step]
        return Ap((ap, ((name, a, b),)))

    def IND(win, off):
        return Ap((win[0].indirect(off[0]), win[1] + off[1]))

    def wait(q, sem, val):
        if known[q].get(sem, 0) >= val:
            return
        queue[q].wait_ge(T.sem[sem], val)
        known[q][sem] = val
        for s, c in snap.get((sem, val), {}).items():
            if known[q].get(s, 0) < c:
                known[q][s] = c

    def deps(q, outs, ins):
        need = {}
        for w, group in ((True, outs), (False, ins)):
            for x in group:
                for name, lo, hi in x[1]:
                    ps = name.startswith("ps")
                    for a in seen.get(name, ()):
                        apart = a[0] >= hi or a[1] <= lo
                        if apart and not ps:
                            continue
                        if a[3] == q:
                            if q == "t" or apart or not (w or a[2]):
                                continue
                        elif not ps and not (w or a[2]):
                            continue
                        need[a[4]] = max(need.get(a[4], 0), a[5])
        for s in sorted(need):
            wait(q, s, need[s])

    def record(q, outs, ins, sem, val):
        k = known.get(q, {})
        for w, group in ((False, ins), (True, outs)):
            for x in group:
                for name, lo, hi in x[1]:
                    lst = seen.setdefault(name, [])
                    if w:
                        lst[:] = [a for a in lst if not (lo <= a[0] and a[1] <= hi and k.get(a[4], 0) >= a[5])]
                    else:
                        lst[:] = [a for a in lst if not (a[3] == q and not a[2] and (a[0], a[1]) == (lo, hi))]
                    lst.append([lo, hi, w, q, sem, val])

    def run(q, outs, ins, call):
        deps(q, outs, ins)
        sem = "q" + q
        count[q] += 1
        snap[(sem, count[q])] = dict(known[q])
        call().then_inc(T.sem[sem], 1)
        record(q, outs, ins, sem, count[q])

    def dma(q, sem, out, in_, outs, ins):
        deps(q, outs, ins)
        snap[(sem, 16)] = dict(known[q])
        queue[q].dma_start(out, in_).then_inc(T.sem[sem], 16)
        record("dma" + sem, outs, ins, sem, 16)

    def landed(name, sem, val):
        record("net" + sem, [A(name)], [], sem, val)

    def isap(s):
        return isinstance(s, Ap)

    def tt(out, a, b, op):
        run("v", [out], [a, b], lambda: g.vector.tensor_tensor(out[0], a[0], b[0], op))

    def ts(out, a, s1, op0, s2=None, op1=None):
        ins = [a] + [s for s in (s1, s2) if isap(s)]
        x1 = s1[0] if isap(s1) else s1
        x2 = s2[0] if isap(s2) else s2
        if op1 is None:
            run("v", [out], ins, lambda: g.vector.tensor_scalar(out[0], a[0], x1, None, op0))
        else:
            run("v", [out], ins, lambda: g.vector.tensor_scalar(out[0], a[0], x1, x2, op0, op1))

    def cp(out, a):
        run("v", [out], [a], lambda: g.vector.tensor_copy(out[0], a[0]))

    def fill(out, x):
        run("v", [out], [], lambda: g.vector.memset(out[0], x))

    def scan(out, d0, d1, op0, op1):
        run("v", [out], [d0, d1], lambda: g.vector.tensor_tensor_scan(out[0], d0[0], d1[0], 0.0, op0, op1))

    def act(out, a, func, bias, scale=1.0):
        run("s", [out], [a], lambda: g.scalar.activation(out[0], a[0], func, bias=bias, scale=scale))

    def actcp(out, a):
        run("s", [out], [a], lambda: g.scalar.activation(out[0], a[0], COPY))

    def mm(out, l, r, start=True, stop=True):
        run("t", [out], [l, r], lambda: g.tensor.matmul(out[0], l[0], r[0], start, stop))

    dma("s", "dS", T["ST0"][:], T.st[:], [A("ST0")], [])
    dma("y", "dX", T["X"][:, 0:W], T.x[:], [A("X", 0, W)], [])
    dma("s", "dL", T["LND0"][:, 64:128], T.sp[:], [A("LND0", 64, 128)], [])
    dma("s", "dC", T["LND0"][:, 0:64], T.ch[:], [A("LND0", 0, 64)], [])
    dma("s", "dW", T["WT"][:], T.wt[:], [A("WT")], [])
    dma("s", "dF", T["F0"][:], T.fl[:], [A("F0")], [])

    def iota(out, pattern, cm):
        run("g", [out], [], lambda: g.iota(out[0], pattern, 0, cm))
    iota(A("PI"), [[1, 1]], 1)
    iota(A("ROW"), [[1, 128]], 0)
    iota(A("KQI"), [[4, 8], [0, 64]], 0)

    def send(t_from, name_to, sem, dst):
        rid, pid, _ = topo.addr(dst)
        deps("g", [], [A(t_from)])
        g.remote_dma(out_ap=T[name_to][:], in_ap=T[t_from][:], remote_sem=T.sem[sem], local_sem=T.sem.loc,
                     pid=pid, routing_id=rid, dma_engine_mask=topo.mask(core, dst))
        return len(topo.engines(core, dst))
    out_total = 0
    for t in range(1, RO):
        out_total += send("ST0", "ST%d" % t, "st%d" % t, T.cores[(rank + t) % n])
        landed("ST%d" % t, "st%d" % t, len(topo.engines(T.cores[(rank - t) % n], core)))

    fill(A("Dm"), 0.0)
    fill(A("Wm"), 0.0)
    ts(A("QI"), A("PI"), 15, AND)
    ts(A("GI"), A("PI"), 4, SHR)
    cp(A("PC"), A("PI"))
    cp(A("ROWF"), A("ROW"))
    cp(A("QC"), A("QI"))
    cp(A("GC"), A("GI"))
    ts(A("CQI"), A("ROW"), 15, AND)
    ts(A("CGI"), A("ROW"), 4, SHR)
    cp(A("CQF"), A("CQI"))
    cp(A("CGF"), A("CGI"))
    ts(A("ID"), A("ROWF"), A("PC"), EQ)
    ts(A("BO"), A("CGF"), A("GC"), EQ)
    ts(A("EQ16"), A("ROWF", 0, 16), A("QC"), EQ)
    ts(A("QC64"), A("QC"), 64.0, MUL)
    ts(A("C16M"), A("QC"), -1.0, MUL, 16.0, ADD)
    fill(A("L0"), 0.0)
    fill(A("RT", 1024, RTW), 0.0)
    ts(A("DP0", 0, 128, 2), A("ROWF", 0, 64), 0.0, MUL, A("EQ16", 0, 1), ADD)
    cp(A("DP0", 1, 128, 2), A("ROWF", 0, 64))
    ts(A("MC"), A("ROWF", 0, 8), -64.0, MUL, A("QC64"), ADD)
    for q in range(16):
        ts(A("GT", q * 128, q * 128 + 128), A("BO"), A("EQ16", q, q + 1), MUL)
    ts(A("R0"), A("ID"), A("EQ16", 0, 1), MUL)
    ts(A("PCL"), A("ROWF", 1, 5), -1.0, MUL, A("PC"), ADD)
    ts(A("PCG"), A("ROWF", 1, 5), -1.0, MUL, A("QC"), ADD)
    ts(A("PCG"), A("PCG"), 0.0, GE, 1000.0, MUL)
    tt(A("PCL"), A("PCL"), A("PCG"), ADD)
    for l in range(1, 5):
        ts(A("shx"), A("ROWF"), 1000.0, ADD, A("PCL", l - 1, l), EQ)
        tt(A("SH%d" % l), A("shx"), A("ID"), SUB)
    for m in range(16):
        actcp(A("Dm", m * 129, m * 128 + 128, 16), A("ID", m, 128, 16))
    ts(A("WB8"), A("BO"), A("WT"), MUL, 8.0, MUL)
    for m in range(16):
        cp(A("Wm", m * 129, m * 128 + 128, 16), A("WB8", 0, 128, 16))
    fill(A("LOG", 0, 64), 0.0)
    fill(A("NEG"), -2048.0)
    fill(A("ONE"), 1.0)
    fill(A("X", W, DUMP), 0.0)

    def late_constants(part):
        if part == 0:
            fill(A("Gm"), 0.0)
        elif part == 1:
            for m in range(16):
                actcp(A("Gm", m * 129, m * 128 + 128, 16), A("BO", 0, 128, 16))
            fill(A("MASK4"), 1.0)
            fill(A("MASK4", 0, 1024, 4), 0.0)
            fill(A("OHL", 0, 64), 0.0)
            fill(A("VB", 1024, 1040), 0.0)
            fill(A("MASK16"), 1.0)
            fill(A("MASK16", 0, 128, 16), 0.0)
            fill(A("M16F"), 1.0)
            fill(A("M16F", 0, 64, 16), 0.0)
            fill(A("ON16"), 0.0625)
        else:
            ts(A("WB1"), A("BO"), A("WT"), MUL)
            ts(A("BO3"), A("BO"), 3.0 / 64, MUL)
            ts(A("BO1"), A("BO"), 1.0 / 64, MUL)
            ts(A("IN1"), A("ID"), -1.0, MUL)
            ts(A("IN2"), A("ID"), -2.0, MUL)
            ts(A("QN4"), A("QC"), -4.0, MUL)
            ts(A("KQ"), A("KQI"), A("QN4"), ADD)
            ts(A("DIAG"), A("CQF", 0, 64), A("QC"), EQ)
            ts(A("OFXC"), A("ROWF", 0, 64), 127.0, MUL, -8192.0, ADD)
            ts(A("I4"), A("ROWF", 0, 4), 16.0, MUL, A("QC"), ADD)
            ts(A("BV4"), A("I4"), 16.0, MUL, 16.0, ADD)
            ts(A("BX4"), A("I4"), 8192.0, ADD)

    def zslot(k, i0, i1):
        if k < 4:
            return A("ZA", 64 * i0 + k, 64 * i1, 4)
        if k < 7:
            return A("ZB", 64 * i0 + k - 3, 64 * i1, 4)
        return A("Z7", 16 * i0, 16 * i1)

    def zcol(k, m):
        if k < 4:
            return A("ZA", 4 * m + k, 4096, 64)
        if k < 7:
            return A("ZB", 4 * m + k - 3, 4096, 64)
        return A("Z7", m, 1024, 16)

    def gz(eng, k, i0, i1):
        eng(zslot(k, i0, i1), IND(A("X", 0, W), A("OFFZ", i0, i1)))

    def gc(eng, k, i0, i1):
        eng(A("CB", 16 * i0, 16 * i1), IND(A("RT", 64 * k, RTW), A("OFFC", i0, i1)))

    def entries():
        act(A("CBF"), A("psC", 0, 64), IDT, 262144.0, 64.0)
        act(A("CA"), A("psC", 0, 64), IDT, 18.5, 0.125)

    def cwrap():
        for m in range(16):
            mm(A("psC", 0, 64), A("Dm", m * 128, m * 128 + 128), A("CB", m, 1024, 16), m == 0, m == 15)
        entries()

    def uwrap(k):
        mm(A("psW", 0, 64), A("NEG"), A("ONE"), True, False)
        for m in range(16):
            mm(A("psW", 0, 64), A("Wm", m * 128, m * 128 + 128), zcol(k, m), False, m == 15)

    def scan1(q):
        scan(A("OA", 1024 * q, 1024 * q + 1024), A("MASK4"), A("ZA", 1024 * q, 1024 * q + 1024), MUL, MAX)

    def scan1copy(q):
        actcp(A("ZB", 1024 * q, 1024 * q + 1024, 4), A("OA", 1024 * q + 3, 1024 * q + 1024, 4))

    def scan2(q):
        scan(A("OB", 1024 * q, 1024 * q + 1024), A("MASK4"), A("ZB", 1024 * q, 1024 * q + 1024), MUL, MAX)

    def arith(k):
        old, nx = "DP%d" % k, "DP%d" % (k + 1)
        tt(A("I1"), A("psW", 0, 64), A("CBF"), ADD)
        if k == 7:
            ts(A("N64"), A("I1"), 192, AND)
            tt(A("LOG", 512, 576), A("LOG", 448, 512), A("N64"), ADD)
            return
        tt(A("psA", 0, 64), A("psW", 0, 64), A("CA"), MUL)
        ts(A("N64"), A("I1"), 192, AND)
        ts(A("DH"), A("I1"), 4, SHR)
        tt(A(nx, 1, 128, 2), A(old, 1, 128, 2), A("N64"), ADD)
        tt(A("YI"), A("psA", 0, 64), A("DH"), ADD)
        ts(A(nx, 0, 128, 2), A(nx, 1, 128, 2), A("MC", k + 1, k + 2), GE)
        scan(A("QS"), A("L0"), A(nx), MUL, ADD)
        ts(A("SI"), A("YI"), 2, SHR, W - 1, AND)
        cp(A("OFFC"), A("QS", 1, 128, 2))
        cp(A("OFFZ"), A("SI"))

    def log(k):
        tt(A("LOG", 64 * (k + 1), 64 * (k + 2)), A("LOG", 64 * k, 64 * (k + 1)), A("N64"), ADD)

    ysn = [0]

    def ysum(cnt):
        for _ in range(cnt):
            c = ysn[0]
            mm(A("psY", 0, 64), A("ID"), A("X", c, W, 128), c == 0, False)
            ysn[0] += 1

    for t in range(RO):
        last = t == RO - 1
        lnd, snd, F = "LND%d" % t, "SND%d" % t, "F%d" % t
        C, L = A(lnd, 0, 64), A(lnd, 64, 128)
        for l in range(1, 5):
            mm(A("psF1", l * 64 - 64, l * 64), A("SH%d" % l), C)
        for q in range(16):
            mm(A("psA" if q < 8 else "psB", (q % 8) * 64, (q % 8) * 64 + 64), A("GT", q * 128, q * 128 + 128), C)
        ts(A("T613"), L, 613.0, MUL)
        tt(A("S0"), A("T613"), A("SA" if t else "ST0"), ADD)
        ts(A("SI"), A("S0"), W - 1, AND)
        cp(A("OFFZ"), A("SI"))
        gz(actcp, 0, 0, Z0_SCALAR)
        for l in range(1, 5):
            ts(A("MK", l * 64 - 64, l * 64), L, float(l), EQ)
        tt(A("CM"), A("MK"), A("psF1", 0, 256), MUL)
        mm(A("psC", 0, 64), A("GT", 0, 128), C, True, False)
        for l in range(1, 5):
            mm(A("psC", 0, 64), A("R0"), A("CM", l * 64 - 64, l * 64), False, l == 4)
        entries()
        actcp(A("RT", 0, 512), A("psA"))
        actcp(A("RT", 512, 1024), A("psB"))
        gz(cp, 0, Z0_SCALAR, 64)
        ts(A("L0", 1, 128, 2), L, 64.0, MUL)
        uwrap(0)
        if t == 0:
            late_constants(0)
        for m in range(16):
            for h in range(2):
                mm(A("psF%d" % h, m, 512, 16), A("ID"), A(F, 32 * h, 32 * h + 32))
        ts(A("PRI"), L, 32.0, MUL, A("C16M"), ADD)
        ts(A("LM15"), L, 15.0, ADD)
        arith(0)
        for k in range(1, 7):
            gc(actcp, k, 0, C_SCALAR)
            gc(cp, k, C_SCALAR, 64)
            gz(actcp, k, 0, Z_SCALAR)
            gz(cp, k, Z_SCALAR, 64)
            log(k - 1)
            cwrap()
            uwrap(k)
            if last:
                ysum(21)
            if k == 3:
                scan1(0)
            elif k == 4:
                scan1(1)
                scan1(2)
                scan1copy(0)
            elif k == 5:
                scan1(3)
                scan1copy(1)
                scan1copy(2)
                scan1copy(3)
            elif k == 6:
                scan2(0)
            elif t == 0:
                late_constants(k)
            arith(k)
        gc(actcp, 7, 0, 64)
        gz(actcp, 7, 0, 64)
        for q in range(1, 4):
            scan2(q)
        log(6)
        cwrap()
        uwrap(7)
        if last:
            ysum(128 - ysn[0])
        for h in range(2):
            o, i = 512 * h, A("OFFZ", 32 * h, 32 * h + 32)
            tt(A("VB", o, o + 512), IND(A("X", 0, W), i), A("OB", 4 * o + 3, 4 * o + 2048, 4), MAX)
        for h in range(2):
            o = 512 * h
            tt(A("GEb", o, o + 512), A("VB", o, o + 512), A("psF%d" % h), GE)
        arith(7)
        for m in range(16):
            mm(A("psA", 0, 64), A("Gm", m * 128, m * 128 + 128), A("GEb", m, 1024, 16), m == 0, m == 15)
        for l in range(1, 5):
            mm(A("psF0", l * 64 - 64, l * 64), A("SH%d" % l), C)
        ts(A("FT"), A("psA", 0, 64), 9.5, GE)
        tt(A("SC"), A("FT"), A("PRI"), MUL)
        run("t", [A("psT", 0, 128)], [A("SC"), A("ID")],
            lambda: g.tensor.transpose(T["psT"][0:64, 0:128], T["SC"][:, 0:64], T["ID"][:]))
        scan(A("SX", 0, 128, 1, 64), A("MASK16", 0, 128, 1, 64), A("psT", 0, 128, 1, 64), MUL, MAX)
        mm(A("psC", 0, 64), A("SX", 0, 128, 1, 64), A("ID", 0, 64, 1, 64))
        cp(A("PX"), A("psC", 0, 64))
        mm(A("psW", 0, 64), A("GT", 15 * 128, 16 * 128), A("PX"))
        tt(A("psA", 0, 64), A("SC"), A("psW", 0, 64), EQ)
        cp(A("BI"), A("psW", 0, 64))
        for h, ps in ((0, "psB"), (1, "psC")):
            o = 256 * h
            mm(A(ps, 0, 256), A("ID"), A("KQ", o, o + 256), True, False)
            for k in range(4 * h + 1, 4 * h + 5):
                tt(A("OHL", 64 * k, 64 * k + 64), A("LOG", 64 * k, 64 * k + 64), A("psA", 0, 64), MUL)
            mm(A(ps, 0, 256), A("BO3"), A("OHL", o, o + 256), False, False)
            mm(A(ps, 0, 256), A("BO1"), A("OHL", o + 64, o + 320), False, True)
        ts(A("MI"), A("BI"), 31, AND)
        ts(A("LI"), A("BI"), 5, SHR)
        ts(A("AT", 0, 256), A("psB", 0, 256), 0.0, MAX, 4.0, MIN)
        act(A("SG", 256, 512), A("psC", 0, 256), SIGN, -3.5)
        act(A("SG", 0, 256), A("psB", 0, 256), SIGN, -3.5)
        ts(A("OK"), A("psW", 0, 64), 0.5, GE)
        ts(A("GG"), A("MI"), A("C16M"), GE)
        ts(A("AT", 256, 512), A("psC", 0, 256), 0.0, MAX, 4.0, MIN)
        tt(A("LE"), A("GG"), A("LI"), MUL)
        mm(A("psW", 0, 64), A("IN1"), A("LM15"), True, False)
        for name, lhs, k0 in (("AT", "ID", 0), ("SG", "IN2", 4), ("SG", "IN2", 0), ("AT", "ID", 4)):
            for k in range(k0, k0 + 4):
                mm(A("psW", 0, 64), A(lhs), A(name, 64 * k, 64 * k + 64), False, (name, k) == ("AT", 7))
        for l in range(1, 5):
            ts(A("MK", l * 64 - 64, l * 64), A("LE"), float(l), EQ)
        tt(A("CM"), A("MK"), A("psF0", 0, 256), MUL)
        mm(A("psF1", 0, 64), A("ID"), C, True, False)
        for l in range(1, 5):
            mm(A("psF1", 0, 64), A("ID"), A("CM", l * 64 - 64, l * 64), False, l == 4)
        tt(A("DL"), A("psW", 0, 64), A("OK"), MUL)
        tt(A(snd, 64, 128), A("DL"), L, ADD)
        actcp(A(snd, 0, 64), A("psF1", 0, 64))
        if not last:
            out_total += send(snd, "LND%d" % (t + 1), "arr%d" % (t + 1), T.cores[(rank + 1) % n])
            landed("LND%d" % (t + 1), "arr%d" % (t + 1), len(topo.engines(T.cores[(rank - 1) % n], core)))
            mm(A("psA", 0, 64), A("ON16"), A("OK"))
        else:
            dma("y", "oL", T.yl[:], T[snd][:, 64:128], [], [A(snd, 64, 128)])
            dma("y", "oC", T.yc[:], T[snd][:, 0:64], [], [A(snd, 0, 64)])
        tt(A("MD"), A("MI"), A("DIAG"), MUL)
        scan(A("SD"), A("M16F"), A("MD"), MUL, ADD)
        tt(A("OKD"), A("OK"), A("DIAG"), MUL)
        tt(A("O4"), A("BV4"), A("SD", 15, 64, 16), SUB)
        cp(A("OV"), A("O4"))
        cp(A("VV"), IND(A("VB"), A("OV")))
        mm(A("psC", 0, 64), A("WB1"), A("VV"))
        tt(A("FVI"), A(F), A("VV"), ADD)
        cp(A("HI"), A("psC", 0, 64))
        ts(A("FH"), A("FVI"), 1, SHR)
        ts(A("HM"), A("HI"), 127, AND)
        tt(A("FD"), A("FH"), A(F), SUB)
        tt(A("X1"), A("HM"), A("OFXC"), ADD)
        tt(A("FE"), A("FD"), A("OK"), MUL)
        tt(A("X2"), A("X1"), A("OKD"), MUL)
        tt(A("F%d" % (t + 1)), A(F), A("FE"), ADD)
        scan(A("SD2"), A("M16F"), A("X2"), MUL, ADD)
        tt(A("O4X"), A("BX4"), A("SD2", 15, 64, 16), ADD)
        cp(A("OX"), A("O4X"))
        if not last:
            run("v", [A("ACOL")], [A("psA", 0, 64)],
                lambda: g.vector.tensor_reduce(T["ACOL"][:], T["psA"][:, 0:64], AxisListType.X, ADD))
            cp(IND(A("X"), A("OX")), A("VV"))
            ts(A("SA"), A("ST%d" % (t + 1)), A("ACOL"), ADD)
        else:
            cp(A("OLD"), IND(A("X"), A("OX")))
            tt(A("PR"), A("VV"), A("OLD"), SUB)
            tt(A("DIF"), A("PR"), A("OK"), MUL)
            mm(A("psY", 0, 64), A("ID"), A("DIF"), False, True)
            cp(A("YS"), A("psY", 0, 64))
            dma("y", "oF", T.yf[:], T["F4"][:], [], [A("F4")])
            dma("y", "oS", T.ys[:], T["YS"][:], [], [A("YS")])

    for q in "vstg":
        wait("g", "q" + q, count[q])
    for s in ("dX", "dW", "dC", "dL", "dS", "dF", "oL", "oC", "oF", "oS"):
        wait("g", s, 16)
    wait("g", "loc", out_total)
    for t in range(1, RO):
        wait("g", "st%d" % t, len(topo.engines(T.cores[(rank - t) % n], core)))
        wait("g", "arr%d" % t, len(topo.engines(T.cores[(rank - 1) % n], core)))
